import numpy as np, ml_dtypes
CORES = [1,129,9,137,17,145,25,153,33,161,41,169,49,177,57,185,65,193,73,201,81,209,89,217,97,225,105,233,113,241,121,249]
N = 32
PERM = [[0,16],[1,17],[2,18],[3,19],[4,20],[5,21],[6,22],[7,23],[8,24],[9,25],[10,26],[11,27],[12,28],[13,29],[14,30],[15,31],[16,0],[17,1],[18,2],[19,3],[20,4],[21,5],[22,6],[23,7],[24,8],[25,9],[26,10],[27,11],[28,12],[29,13],[30,14],[31,15]]
def setup_inputs(rng):
    return {"x": rng.standard_normal((N, 128, 256), dtype=np.float32).astype(ml_dtypes.bfloat16)}
def reference(x):
    y = np.empty_like(x)
    for s, d in PERM:
        y[d] = x[s]
    return {"y": y}

import comms_topo

SCRATCH = {
    "send": ("dram", [128, 256], "bfloat16"),
    "land": ("dram", [128, 256], "bfloat16"),
}
SEMAPHORES = ["loaded", "left", "arrived", "stored"]


def rank_program(g, core, T, topo):
    rank = T.rank_of(core)
    if rank is None:
        return
    dst = {s: d for s, d in T.tables["PERM"]}[rank]
    dcore = T.cores[dst]

    if dcore == core:
        g.sync.dma_start(T.y[:], T.x[:]).then_inc(T.sem.stored, 16)
        g.wait_ge(T.sem.stored, 16)
        return

    assert topo.may_write(core, dcore)
    rid, pid = topo.addr(dcore, core)
    mask = topo.mask(core, dcore)
    engines = bin(mask).count("1")

    g.sync.dma_start(T.send[:], T.x[:]).then_inc(T.sem.loaded, 16)

    g.wait_ge(T.sem.loaded, 16)
    g.remote_dma(T.land[:], T.send[:], T.sem.arrived, T.sem.left, pid, rid, mask)

    g.scalar.wait_ge(T.sem.arrived, engines)
    g.scalar.dma_start(T.y[:], T.land[:]).then_inc(T.sem.stored, 16)

    g.wait_ge(T.sem.left, engines)
    g.wait_ge(T.sem.stored, 16)
